import numpy as np
import ml_dtypes


def mxq(x, axis, fmt="e4m3"):
    dtype, down = {"e4m3": (ml_dtypes.float8_e4m3fn, 7), "e5m2": (ml_dtypes.float8_e5m2, 14)}[fmt]
    v = np.moveaxis(np.asarray(x, np.float32).astype(ml_dtypes.bfloat16).astype(np.float64), axis, -1)
    blocks = v.reshape(v.shape[:-1] + (-1, 32))
    amax = np.abs(blocks).max(-1, keepdims=True)
    byte = np.maximum(np.where(amax > 0, np.frexp(amax)[1] - 1 + 127, 0) - down, 1)
    scale = np.exp2(byte - 127.0)
    codes = (blocks / scale).astype(np.float32).astype(dtype).astype(np.float64)
    return np.moveaxis((codes * scale).reshape(v.shape), -1, axis)


WIDE = False


def mx_kscale(k):
    if not WIDE:
        return np.ones(k)
    levels = np.array([30, -30])
    if k % 512:
        return np.exp2(np.random.permutation(np.resize(levels, k // 32))).repeat(32)
    a = np.empty((k // 512, 16))
    for p in range(k // 512):
        a[p, :8] = np.random.permutation(np.resize(levels, 8))
        for g in range(8):
            far = levels[np.abs(levels - a[p, g]) >= 10]
            a[p, g + 8] = far[np.random.randint(len(far))]
    return np.exp2(a.ravel()).repeat(32)


def f64(x):
    return np.asarray(x).astype(np.float64)


def striped(idx):
    return np.tile(np.asarray(idx).reshape(-1, 16).T, (8, 1)).astype(np.uint16)


def unstriped(offs):
    return offs[:16].T.reshape(-1).astype(np.int64)


K, T, J, I, V = 1024, 1024, 256, 256, 1024


def setup_inputs():
    n = np.random.standard_normal
    idx = np.random.permutation(T)[:J]
    idx2 = np.random.permutation(T)[:J]
    idx3 = np.random.permutation(V)[:I]
    fk = mx_kscale(K)
    return {
        "xf": (n((K, T)) * 0.03).astype(np.float32),
        "fk": (np.random.uniform(0.5, 2.0, (K, 1)) * fk[:, None]).astype(np.float32),
        "kf": (n((K, V))).astype(np.float32),
        "ko": (n((K, I)) * 0.6).astype(np.float32),
        "fi": (np.random.uniform(0.5, 2.0, (K, 1)) / fk[:, None]).astype(np.float32),
        "bi": (np.random.uniform(-0.7, 0.7, (1, I))).astype(np.float32),
        "offs": striped(idx),
        "offs2": striped(idx2),
        "offs3": striped(idx3),
    }


def reference(xf, fk, kf, ko, fi, bi, offs, offs2, offs3):
    idx = unstriped(offs)
    idx2 = unstriped(offs2)
    idx3 = unstriped(offs3)
    u = (f64(xf)[:, idx] - f64(xf)[:, idx2]) * f64(fk)
    vk = (f64(kf)[:, idx3] + f64(ko)) * f64(fi)
    uq = mxq(u, 0, "e5m2")
    vkq = mxq(vk, 0, "e5m2")
    a0 = uq.T @ vkq
    a = a0 + f64(bi)
    mn = np.mean(a, axis=1, keepdims=True)
    y = np.maximum(a - mn, 0.0)
    return y

@@ -1,0 +1,162 @@
+from contextlib import ExitStack
+
+import concourse.mybir as mybir
+from concourse.masks import make_identity
+
+K, T, J, I, V = 1024, 1024, 256, 256, 1024
+FLOPS = 2 * K * J * I
+
+F32 = mybir.dt.float32
+BF16 = mybir.dt.bfloat16
+U32 = mybir.dt.uint32
+U16 = mybir.dt.uint16
+U8 = mybir.dt.uint8
+E5M2X4 = mybir.dt.float8_e5m2_x4
+ALU = mybir.AluOpType
+ACT = mybir.ActivationFunctionType
+
+P = 128
+PACK = 4
+PASSES = K // (P * PACK)
+BI_ROW = 2 * PASSES
+KEPT = 8
+HALF = I // 2
+LAST_ORDER = (2, 0, 1, 3)
+
+
+def tile_list_scores_gaps_mixed_abovemean_f_kernel(tc, xf, fk, kf, ko, fi, bi, offs, offs2, offs3, out):
+    nc = tc.nc
+    with ExitStack() as ctx:
+        keep = ctx.enter_context(tc.tile_pool(name="keep", bufs=1))
+        ring = ctx.enter_context(tc.tile_pool(name="ring", bufs=8))
+        psum = ctx.enter_context(tc.psum_pool(name="psum", bufs=1))
+
+        x_rows = xf.rearrange("(a p t) n -> a t p n", a=PASSES, t=PACK)
+        k_rows = kf.rearrange("(a p t) n -> a t p n", a=PASSES, t=PACK)
+        own_rows = ko.rearrange("(a p t) n -> a p t n", a=PASSES, t=PACK)
+
+        list1 = keep.tile([P, J // 16], U16, name="list1")
+        list2 = keep.tile([P, J // 16], U16, name="list2")
+        list3 = keep.tile([P, I // 16], U16, name="list3")
+        rows_sb = keep.tile([P, P * PACK], F32, name="rows_sb")
+        nc.gpsimd.memset(rows_sb[:], 0.0)
+        nc.scalar.dma_start(out=rows_sb[0:PASSES, :], in_=fk.rearrange("(a n) o -> a (n o)", a=PASSES))
+        nc.scalar.dma_start(out=rows_sb[PASSES : 2 * PASSES, :], in_=fi.rearrange("(a n) o -> a (n o)", a=PASSES))
+        nc.scalar.dma_start(out=rows_sb[BI_ROW : BI_ROW + 1, 0:I], in_=bi)
+
+        slabs = [(a, t) for a in range(PASSES) for t in range(PACK)]
+        x_sb = {s: keep.tile([P, T], F32, name=f"x_{s[0]}_{s[1]}") for s in slabs}
+        k_sb = {s: keep.tile([P, V], F32, name=f"k_{s[0]}_{s[1]}") for s in slabs}
+        own_sb = [keep.tile([P, PACK, I], F32, name=f"own_{a}") for a in range(PASSES)]
+
+        for a, t in slabs:
+            nc.sync.dma_start(out=x_sb[a, t][:], in_=x_rows[a, t])
+            if (a, t) == (0, 0):
+                nc.sync.dma_start(list2[:], offs2)
+                nc.sync.dma_start(list1[:], offs)
+                nc.sync.dma_start(list3[:], offs3)
+        for a in range(PASSES):
+            nc.sync.dma_start(out=own_sb[a][:], in_=own_rows[a])
+            for t in LAST_ORDER if a == PASSES - 1 else range(PACK):
+                nc.sync.dma_start(out=k_sb[a, t][:], in_=k_rows[a, t])
+
+        ident = keep.tile([P, P], F32, name="ident")
+        make_identity(nc, ident[:])
+        turn_bank = psum.tile([P, PACK, P], F32, name="turn_bank")
+        for t in range(PACK):
+            nc.tensor.transpose(turn_bank[:, t, :], rows_sb[:, t : P * PACK : PACK], ident[:])
+        cols_sb = keep.tile([P, PACK, KEPT], F32, name="cols_sb")
+        nc.vector.tensor_copy(cols_sb[:], turn_bank[:, :, 0:KEPT])
+        bi_bank = psum.tile([P, PACK, P], F32, name="bi_bank")
+        for t in range(PACK):
+            nc.tensor.transpose(bi_bank[:, t, :], cols_sb[:, t, BI_ROW : BI_ROW + 1].to_broadcast([P, P]), ident[:])
+
+        def scale_into(woven, values, factor, t):
+            if t < PACK // 2:
+                nc.scalar.activation(woven[:, :, t], values[:], ACT.Copy, scale=factor)
+            else:
+                nc.vector.tensor_scalar(woven[:, :, t], values[:], factor, None, ALU.mult)
+
+        def weave(woven, flat):
+            nc.scalar.copy(
+                woven[:].rearrange("p (c i) t -> p c t i", i=4), flat[:].rearrange("p t (c i) -> p c t i", i=4)
+            )
+
+        def quantise(woven, name):
+            width = woven.shape[1]
+            codes = keep.tile([P, width], U32, name=name + "_codes", align_bytes=64)
+            scales = keep.tile([P, width], U8, name=name + "_scales", align_bytes=64)
+            nc.vector.quantize_mx(
+                out=codes[:].bitcast(E5M2X4), scales=scales[:], in_=woven[:].rearrange("p n t -> p (n t)")
+            )
+            return codes, scales
+
+        u_mx = []
+        for a in range(PASSES):
+            flat = keep.tile([P, PACK, J], BF16, name=f"u_flat_{a}")
+            for t in range(PACK):
+                second = ring.tile([P, J], F32, name="second")
+                nc.scalar.activation(second[:], x_sb[a, t][:].indirect(list2[:]), ACT.Copy)
+                gap = ring.tile([P, J], F32, name="gap")
+                nc.vector.tensor_tensor(gap[:], x_sb[a, t][:].indirect(list1[:]), second[:], ALU.subtract)
+                nc.scalar.activation(flat[:, t, :], gap[:], ACT.Copy, scale=cols_sb[:, t, a : a + 1])
+            woven = keep.tile([P, J, PACK], BF16, name=f"u_woven_{a}", align_bytes=64)
+            weave(woven, flat)
+            u_mx.append(quantise(woven, f"u_{a}"))
+
+        bias = keep.tile([P, I // PACK, PACK], F32, name="bias")
+        nc.scalar.activation(
+            bias[:], bi_bank[:, :, 0 : I // PACK].rearrange("p t n -> p n t"), ACT.Copy, scale=-1.0 / I
+        )
+
+        banks = [psum.tile([P, I], F32, name=f"bank_{h}") for h in range(J // P)]
+        for a in range(PASSES):
+            last = a == PASSES - 1
+            width = HALF if last else I
+            starts = range(0, I, width)
+            woven = {c: keep.tile([P, width, PACK], BF16, name=f"v_woven_{a}_{c}", align_bytes=64) for c in starts}
+            if not last:
+                flat = keep.tile([P, PACK, I], BF16, name=f"v_flat_{a}")
+            for t in LAST_ORDER if last else range(PACK):
+                keys = {}
+                for c in starts:
+                    keys[c] = ring.tile([P, width], F32, name="key")
+                    nc.vector.tensor_tensor(
+                        keys[c][:],
+                        k_sb[a, t][:].indirect(list3[:, c // 16 : (c + width) // 16]),
+                        own_sb[a][:, t, c : c + width],
+                        ALU.add,
+                    )
+                factor = cols_sb[:, t, PASSES + a : PASSES + a + 1]
+                for c in starts:
+                    if last:
+                        scale_into(woven[c], keys[c], factor, t)
+                    else:
+                        nc.scalar.activation(flat[:, t, :], keys[c][:], ACT.Copy, scale=factor)
+            if not last:
+                weave(woven[0], flat)
+            u_codes, u_scales = u_mx[a]
+            for c in starts:
+                v_codes, v_scales = quantise(woven[c], f"v_{a}_{c}")
+                for h in range(J // P):
+                    rows = slice(h * P, (h + 1) * P)
+                    nc.tensor.matmul_mx(
+                        out=banks[h][:, c : c + width],
+                        lhsT=u_codes[:, rows].bitcast(E5M2X4),
+                        lhsT_scale=u_scales[:, rows],
+                        rhs=v_codes[:].bitcast(E5M2X4),
+                        rhs_scale=v_scales[:],
+                        start=(a == 0),
+                        stop=(last and c + width == I),
+                    )
+
+        for h in range(J // P):
+            shrunk = keep.tile([P, I], F32, name=f"shrunk_{h}")
+            neg_mean = keep.tile([P, 1], F32, name=f"neg_mean_{h}")
+            nc.vector.scalar_tensor_tensor(
+                shrunk[:], banks[h][:], -1.0 / I, bias[:].rearrange("p n t -> p (n t)"),
+                ALU.mult, ALU.add, accum_out=neg_mean[:],
+            )
+            result = keep.tile([P, I], F32, name=f"result_{h}")
+            nc.scalar.activation(result[:], shrunk[:], ACT.Relu, bias=neg_mean[:], scale=-float(I))
+            nc.sync.dma_start(out=out[h * P : (h + 1) * P, :], in_=result[:])

@@ -21,6 +21,7 @@ PASSES = K // (P * PACK)
 BI_ROW = 2 * PASSES
 KEPT = 8
 HALF = I // 2
+RUN = 4
 LAST_ORDER = (2, 0, 1, 3)
 
 
@@ -71,17 +72,6 @@ def tile_list_scores_gaps_mixed_abovemean_f_kernel(tc, xf, fk, kf, ko, fi, bi, o
         for t in range(PACK):
             nc.tensor.transpose(bi_bank[:, t, :], cols_sb[:, t, BI_ROW : BI_ROW + 1].to_broadcast([P, P]), ident[:])
 
-        def scale_into(woven, values, factor, t):
-            if t < PACK // 2:
-                nc.scalar.activation(woven[:, :, t], values[:], ACT.Copy, scale=factor)
-            else:
-                nc.vector.tensor_scalar(woven[:, :, t], values[:], factor, None, ALU.mult)
-
-        def weave(woven, flat):
-            nc.scalar.copy(
-                woven[:].rearrange("p (c i) t -> p c t i", i=4), flat[:].rearrange("p t (c i) -> p c t i", i=4)
-            )
-
         def quantise(woven, name):
             width = woven.shape[1]
             codes = keep.tile([P, width], U32, name=name + "_codes", align_bytes=64)
@@ -93,15 +83,19 @@ def tile_list_scores_gaps_mixed_abovemean_f_kernel(tc, xf, fk, kf, ko, fi, bi, o
 
         u_mx = []
         for a in range(PASSES):
-            flat = keep.tile([P, PACK, J], BF16, name=f"u_flat_{a}")
+            gaps = keep.tile([P, PACK, J], F32, name=f"gaps_{a}")
             for t in range(PACK):
                 second = ring.tile([P, J], F32, name="second")
                 nc.scalar.activation(second[:], x_sb[a, t][:].indirect(list2[:]), ACT.Copy)
-                gap = ring.tile([P, J], F32, name="gap")
-                nc.vector.tensor_tensor(gap[:], x_sb[a, t][:].indirect(list1[:]), second[:], ALU.subtract)
-                nc.scalar.activation(flat[:, t, :], gap[:], ACT.Copy, scale=cols_sb[:, t, a : a + 1])
+                nc.vector.tensor_tensor(gaps[:, t, :], x_sb[a, t][:].indirect(list1[:]), second[:], ALU.subtract)
             woven = keep.tile([P, J, PACK], BF16, name=f"u_woven_{a}", align_bytes=64)
-            weave(woven, flat)
+            factors = cols_sb[:, :, a : a + 1].unsqueeze(1).to_broadcast([P, J // RUN, PACK, RUN])
+            nc.vector.tensor_tensor(
+                woven[:].rearrange("p (c i) t -> p c t i", i=RUN),
+                gaps[:].rearrange("p t (c i) -> p c t i", i=RUN),
+                factors,
+                ALU.mult,
+            )
             u_mx.append(quantise(woven, f"u_{a}"))
 
         bias = keep.tile([P, I // PACK, PACK], F32, name="bias")
@@ -115,8 +109,6 @@ def tile_list_scores_gaps_mixed_abovemean_f_kernel(tc, xf, fk, kf, ko, fi, bi, o
             width = HALF if last else I
             starts = range(0, I, width)
             woven = {c: keep.tile([P, width, PACK], BF16, name=f"v_woven_{a}_{c}", align_bytes=64) for c in starts}
-            if not last:
-                flat = keep.tile([P, PACK, I], BF16, name=f"v_flat_{a}")
             for t in LAST_ORDER if last else range(PACK):
                 keys = {}
                 for c in starts:
@@ -129,12 +121,10 @@ def tile_list_scores_gaps_mixed_abovemean_f_kernel(tc, xf, fk, kf, ko, fi, bi, o
                     )
                 factor = cols_sb[:, t, PASSES + a : PASSES + a + 1]
                 for c in starts:
-                    if last:
-                        scale_into(woven[c], keys[c], factor, t)
+                    if last and t >= PACK // 2:
+                        nc.vector.tensor_scalar(woven[c][:, :, t], keys[c][:], factor, None, ALU.mult)
                     else:
-                        nc.scalar.activation(flat[:, t, :], keys[c][:], ACT.Copy, scale=factor)
-            if not last:
-                weave(woven[0], flat)
+                        nc.scalar.activation(woven[c][:, :, t], keys[c][:], ACT.Copy, scale=factor)
             u_codes, u_scales = u_mx[a]
             for c in starts:
                 v_codes, v_scales = quantise(woven[c], f"v_{a}_{c}")

@@ -32,7 +32,8 @@ def tile_list_scores_gaps_mixed_abovemean_f_kernel(tc, xf, fk, kf, ko, fi, bi, o
         ring = ctx.enter_context(tc.tile_pool(name="ring", bufs=8))
         psum = ctx.enter_context(tc.psum_pool(name="psum", bufs=1))
 
-        x_rows = xf.rearrange("(a p t) n -> a t p n", a=PASSES, t=PACK)
+        x_pairs = xf.rearrange("(a p g e) n -> a g p (e n)", a=PASSES, g=2, e=2)
+        k_pairs = kf.rearrange("(a p g e) n -> a g p (e n)", a=PASSES, g=2, e=2)
         k_rows = kf.rearrange("(a p t) n -> a t p n", a=PASSES, t=PACK)
         own_rows = ko.rearrange("(a p t) n -> a p t n", a=PASSES, t=PACK)
 
@@ -41,25 +42,32 @@ def tile_list_scores_gaps_mixed_abovemean_f_kernel(tc, xf, fk, kf, ko, fi, bi, o
         list3 = keep.tile([P, I // 16], U16, name="list3")
         rows_sb = keep.tile([P, P * PACK], F32, name="rows_sb")
         nc.gpsimd.memset(rows_sb[:], 0.0)
-        nc.scalar.dma_start(out=rows_sb[0:PASSES, :], in_=fk.rearrange("(a n) o -> a (n o)", a=PASSES))
-        nc.scalar.dma_start(out=rows_sb[PASSES : 2 * PASSES, :], in_=fi.rearrange("(a n) o -> a (n o)", a=PASSES))
-        nc.scalar.dma_start(out=rows_sb[BI_ROW : BI_ROW + 1, 0:I], in_=bi)
 
-        slabs = [(a, t) for a in range(PASSES) for t in range(PACK)]
-        x_sb = {s: keep.tile([P, T], F32, name=f"x_{s[0]}_{s[1]}") for s in slabs}
-        k_sb = {s: keep.tile([P, V], F32, name=f"k_{s[0]}_{s[1]}") for s in slabs}
+        warm_in = keep.tile([P, 1], F32, name="warm_in")
+        warm_out = keep.tile([P, 1], F32, name="warm_out")
+        nc.vector.memset(warm_in[:], 0.0)
+        nc.scalar.activation(warm_out[:], warm_in[:], ACT.Copy)
+
+        x_sb = {(a, g): keep.tile([P, 2 * T], F32, name=f"x_{a}_{g}") for a in range(PASSES) for g in range(2)}
+        k_first = [keep.tile([P, 2 * V], F32, name=f"k_first_{g}") for g in range(2)]
+        k_last = [keep.tile([P, V], F32, name=f"k_last_{t}") for t in range(PACK)]
         own_sb = [keep.tile([P, PACK, I], F32, name=f"own_{a}") for a in range(PASSES)]
 
-        for a, t in slabs:
-            nc.sync.dma_start(out=x_sb[a, t][:], in_=x_rows[a, t])
-            if (a, t) == (0, 0):
+        for a, g in x_sb:
+            nc.sync.dma_start(out=x_sb[a, g][:], in_=x_pairs[a, g])
+            if (a, g) == (0, 0):
                 nc.sync.dma_start(list2[:], offs2)
                 nc.sync.dma_start(list1[:], offs)
-                nc.sync.dma_start(list3[:], offs3)
-        for a in range(PASSES):
-            nc.sync.dma_start(out=own_sb[a][:], in_=own_rows[a])
-            for t in LAST_ORDER if a == PASSES - 1 else range(PACK):
-                nc.sync.dma_start(out=k_sb[a, t][:], in_=k_rows[a, t])
+                nc.sync.dma_start(out=rows_sb[0:PASSES, :], in_=fk.rearrange("(a n) o -> a (n o)", a=PASSES))
+                nc.sync.dma_start(out=rows_sb[PASSES : 2 * PASSES, :], in_=fi.rearrange("(a n) o -> a (n o)", a=PASSES))
+                nc.sync.dma_start(out=rows_sb[BI_ROW : BI_ROW + 1, 0:I], in_=bi)
+        nc.sync.dma_start(list3[:], offs3)
+        nc.sync.dma_start(out=own_sb[0][:], in_=own_rows[0])
+        for g in range(2):
+            nc.sync.dma_start(out=k_first[g][:], in_=k_pairs[0, g])
+        nc.sync.dma_start(out=own_sb[1][:], in_=own_rows[1])
+        for t in LAST_ORDER:
+            nc.sync.dma_start(out=k_last[t][:], in_=k_rows[1, t])
 
         ident = keep.tile([P, P], F32, name="ident")
         make_identity(nc, ident[:])
@@ -81,22 +89,33 @@ def tile_list_scores_gaps_mixed_abovemean_f_kernel(tc, xf, fk, kf, ko, fi, bi, o
             )
             return codes, scales
 
+        def pick(window, offsets):
+            picked = ring.tile([P, offsets.shape[1] * 16], F32, name="picked")
+            nc.scalar.activation(picked[:], window.indirect(offsets[:]), ACT.Copy)
+            return picked
+
+        def scale_weave_quantise(values, column, name):
+            width = values.shape[2]
+            woven = keep.tile([P, width, PACK], BF16, name=name + "_woven", align_bytes=64)
+            nc.vector.tensor_tensor(
+                woven[:].rearrange("p (c i) t -> p c t i", i=RUN),
+                values[:].rearrange("p t (c i) -> p c t i", i=RUN),
+                cols_sb[:, :, column : column + 1].unsqueeze(1).to_broadcast([P, width // RUN, PACK, RUN]),
+                ALU.mult,
+            )
+            return quantise(woven, name)
+
         u_mx = []
         for a in range(PASSES):
             gaps = keep.tile([P, PACK, J], F32, name=f"gaps_{a}")
-            for t in range(PACK):
-                second = ring.tile([P, J], F32, name="second")
-                nc.scalar.activation(second[:], x_sb[a, t][:].indirect(list2[:]), ACT.Copy)
-                nc.vector.tensor_tensor(gaps[:, t, :], x_sb[a, t][:].indirect(list1[:]), second[:], ALU.subtract)
-            woven = keep.tile([P, J, PACK], BF16, name=f"u_woven_{a}", align_bytes=64)
-            factors = cols_sb[:, :, a : a + 1].unsqueeze(1).to_broadcast([P, J // RUN, PACK, RUN])
-            nc.vector.tensor_tensor(
-                woven[:].rearrange("p (c i) t -> p c t i", i=RUN),
-                gaps[:].rearrange("p t (c i) -> p c t i", i=RUN),
-                factors,
-                ALU.mult,
-            )
-            u_mx.append(quantise(woven, f"u_{a}"))
+            for g in range(2):
+                pair = x_sb[a, g]
+                second = pick(pair[:, 0:T], list2)
+                nc.vector.tensor_tensor(gaps[:, 2 * g, :], pair[:].indirect(list1[:]), second[:], ALU.subtract)
+                second = pick(pair[:, T : 2 * T], list2)
+                first = pick(pair[:, T : 2 * T], list1)
+                nc.vector.tensor_tensor(gaps[:, 2 * g + 1, :], first[:], second[:], ALU.subtract)
+            u_mx.append(scale_weave_quantise(gaps, a, f"u_{a}"))
 
         bias = keep.tile([P, I // PACK, PACK], F32, name="bias")
         nc.scalar.activation(
@@ -104,41 +123,50 @@ def tile_list_scores_gaps_mixed_abovemean_f_kernel(tc, xf, fk, kf, ko, fi, bi, o
         )
 
         banks = [psum.tile([P, I], F32, name=f"bank_{h}") for h in range(J // P)]
-        for a in range(PASSES):
-            last = a == PASSES - 1
-            width = HALF if last else I
-            starts = range(0, I, width)
-            woven = {c: keep.tile([P, width, PACK], BF16, name=f"v_woven_{a}_{c}", align_bytes=64) for c in starts}
-            for t in LAST_ORDER if last else range(PACK):
-                keys = {}
-                for c in starts:
-                    keys[c] = ring.tile([P, width], F32, name="key")
-                    nc.vector.tensor_tensor(
-                        keys[c][:],
-                        k_sb[a, t][:].indirect(list3[:, c // 16 : (c + width) // 16]),
-                        own_sb[a][:, t, c : c + width],
-                        ALU.add,
-                    )
-                factor = cols_sb[:, t, PASSES + a : PASSES + a + 1]
-                for c in starts:
-                    if last and t >= PACK // 2:
-                        nc.vector.tensor_scalar(woven[c][:, :, t], keys[c][:], factor, None, ALU.mult)
-                    else:
-                        nc.scalar.activation(woven[c][:, :, t], keys[c][:], ACT.Copy, scale=factor)
+
+        def multiply(a, v_mx, cols, start, stop):
             u_codes, u_scales = u_mx[a]
+            v_codes, v_scales = v_mx
+            for h in range(J // P):
+                rows = slice(h * P, (h + 1) * P)
+                nc.tensor.matmul_mx(
+                    out=banks[h][:, cols],
+                    lhsT=u_codes[:, rows].bitcast(E5M2X4),
+                    lhsT_scale=u_scales[:, rows],
+                    rhs=v_codes[:].bitcast(E5M2X4),
+                    rhs_scale=v_scales[:],
+                    start=start,
+                    stop=stop,
+                )
+
+        keys = keep.tile([P, PACK, I], F32, name="keys")
+        for g in range(2):
+            pair = k_first[g]
+            nc.vector.tensor_tensor(keys[:, 2 * g, :], pair[:].indirect(list3[:]), own_sb[0][:, 2 * g, :], ALU.add)
+            listed = pick(pair[:, V : 2 * V], list3)
+            nc.vector.tensor_tensor(keys[:, 2 * g + 1, :], listed[:], own_sb[0][:, 2 * g + 1, :], ALU.add)
+        multiply(0, scale_weave_quantise(keys, PASSES, "v_0"), slice(0, I), True, False)
+
+        starts = range(0, I, HALF)
+        woven = {c: keep.tile([P, HALF, PACK], BF16, name=f"v_1_woven_{c}", align_bytes=64) for c in starts}
+        for t in LAST_ORDER:
+            halves = {}
             for c in starts:
-                v_codes, v_scales = quantise(woven[c], f"v_{a}_{c}")
-                for h in range(J // P):
-                    rows = slice(h * P, (h + 1) * P)
-                    nc.tensor.matmul_mx(
-                        out=banks[h][:, c : c + width],
-                        lhsT=u_codes[:, rows].bitcast(E5M2X4),
-                        lhsT_scale=u_scales[:, rows],
-                        rhs=v_codes[:].bitcast(E5M2X4),
-                        rhs_scale=v_scales[:],
-                        start=(a == 0),
-                        stop=(last and c + width == I),
-                    )
+                halves[c] = ring.tile([P, HALF], F32, name="half")
+                nc.vector.tensor_tensor(
+                    halves[c][:],
+                    k_last[t][:].indirect(list3[:, c // 16 : (c + HALF) // 16]),
+                    own_sb[1][:, t, c : c + HALF],
+                    ALU.add,
+                )
+            factor = cols_sb[:, t, PASSES + 1 : PASSES + 2]
+            for c in starts:
+                if t >= PACK // 2:
+                    nc.vector.tensor_scalar(woven[c][:, :, t], halves[c][:], factor, None, ALU.mult)
+                else:
+                    nc.scalar.activation(woven[c][:, :, t], halves[c][:], ACT.Copy, scale=factor)
+        for c in starts:
+            multiply(1, quantise(woven[c], f"v_1_{c}"), slice(c, c + HALF), False, c + HALF == I)
 
         for h in range(J // P):
             shrunk = keep.tile([P, I], F32, name=f"shrunk_{h}")

@@ -43,11 +43,6 @@ def tile_list_scores_gaps_mixed_abovemean_f_kernel(tc, xf, fk, kf, ko, fi, bi, o
         rows_sb = keep.tile([P, P * PACK], F32, name="rows_sb")
         nc.gpsimd.memset(rows_sb[:], 0.0)
 
-        warm_in = keep.tile([P, 1], F32, name="warm_in")
-        warm_out = keep.tile([P, 1], F32, name="warm_out")
-        nc.vector.memset(warm_in[:], 0.0)
-        nc.scalar.activation(warm_out[:], warm_in[:], ACT.Copy)
-
         x_sb = {(a, g): keep.tile([P, 2 * T], F32, name=f"x_{a}_{g}") for a in range(PASSES) for g in range(2)}
         k_first = [keep.tile([P, 2 * V], F32, name=f"k_first_{g}") for g in range(2)]
         k_last = [keep.tile([P, V], F32, name=f"k_last_{t}") for t in range(PACK)]

from contextlib import ExitStack

import concourse.mybir as mybir
from concourse.masks import make_identity

K, T, J, I, V = 1024, 1024, 256, 256, 1024
FLOPS = 2 * K * J * I

F32 = mybir.dt.float32
BF16 = mybir.dt.bfloat16
U32 = mybir.dt.uint32
U16 = mybir.dt.uint16
U8 = mybir.dt.uint8
E5M2X4 = mybir.dt.float8_e5m2_x4
ALU = mybir.AluOpType
ACT = mybir.ActivationFunctionType

P = 128
PACK = 4
PASSES = K // (P * PACK)
BI_ROW = 2 * PASSES
KEPT = 8
HALF = I // 2
RUN = 4
LAST_ORDER = (2, 0, 1, 3)


def tile_list_scores_gaps_mixed_abovemean_f_kernel(tc, xf, fk, kf, ko, fi, bi, offs, offs2, offs3, out):
    nc = tc.nc
    with ExitStack() as ctx:
        keep = ctx.enter_context(tc.tile_pool(name="keep", bufs=1))
        ring = ctx.enter_context(tc.tile_pool(name="ring", bufs=8))
        psum = ctx.enter_context(tc.psum_pool(name="psum", bufs=1))

        x_pairs = xf.rearrange("(a p g e) n -> a g p (e n)", a=PASSES, g=2, e=2)
        k_pairs = kf.rearrange("(a p g e) n -> a g p (e n)", a=PASSES, g=2, e=2)
        k_rows = kf.rearrange("(a p t) n -> a t p n", a=PASSES, t=PACK)
        own_rows = ko.rearrange("(a p t) n -> a p t n", a=PASSES, t=PACK)

        list1 = keep.tile([P, J // 16], U16, name="list1")
        list2 = keep.tile([P, J // 16], U16, name="list2")
        list3 = keep.tile([P, I // 16], U16, name="list3")
        rows_sb = keep.tile([P, P * PACK], F32, name="rows_sb")
        nc.gpsimd.memset(rows_sb[:], 0.0)

        x_sb = {(a, g): keep.tile([P, 2 * T], F32, name=f"x_{a}_{g}") for a in range(PASSES) for g in range(2)}
        k_first = [keep.tile([P, 2 * V], F32, name=f"k_first_{g}") for g in range(2)]
        k_last = [keep.tile([P, V], F32, name=f"k_last_{t}") for t in range(PACK)]
        own_sb = [keep.tile([P, PACK, I], F32, name=f"own_{a}") for a in range(PASSES)]

        for a, g in x_sb:
            nc.sync.dma_start(out=x_sb[a, g][:], in_=x_pairs[a, g])
            if (a, g) == (0, 0):
                nc.sync.dma_start(list2[:], offs2)
                nc.sync.dma_start(list1[:], offs)
                nc.sync.dma_start(out=rows_sb[0:PASSES, :], in_=fk.rearrange("(a n) o -> a (n o)", a=PASSES))
                nc.sync.dma_start(out=rows_sb[PASSES : 2 * PASSES, :], in_=fi.rearrange("(a n) o -> a (n o)", a=PASSES))
                nc.sync.dma_start(out=rows_sb[BI_ROW : BI_ROW + 1, 0:I], in_=bi)
        nc.sync.dma_start(list3[:], offs3)
        nc.sync.dma_start(out=own_sb[0][:], in_=own_rows[0])
        for g in range(2):
            nc.sync.dma_start(out=k_first[g][:], in_=k_pairs[0, g])
        nc.sync.dma_start(out=own_sb[1][:], in_=own_rows[1])
        for t in LAST_ORDER:
            nc.sync.dma_start(out=k_last[t][:], in_=k_rows[1, t])

        ident = keep.tile([P, P], F32, name="ident")
        make_identity(nc, ident[:])
        turn_bank = psum.tile([P, PACK, P], F32, name="turn_bank")
        for t in range(PACK):
            nc.tensor.transpose(turn_bank[:, t, :], rows_sb[:, t : P * PACK : PACK], ident[:])
        cols_sb = keep.tile([P, PACK, KEPT], F32, name="cols_sb")
        nc.vector.tensor_copy(cols_sb[:], turn_bank[:, :, 0:KEPT])
        bi_bank = psum.tile([P, PACK, P], F32, name="bi_bank")
        for t in range(PACK):
            nc.tensor.transpose(bi_bank[:, t, :], cols_sb[:, t, BI_ROW : BI_ROW + 1].to_broadcast([P, P]), ident[:])

        def quantise(woven, name):
            width = woven.shape[1]
            codes = keep.tile([P, width], U32, name=name + "_codes", align_bytes=64)
            scales = keep.tile([P, width], U8, name=name + "_scales", align_bytes=64)
            nc.vector.quantize_mx(
                out=codes[:].bitcast(E5M2X4), scales=scales[:], in_=woven[:].rearrange("p n t -> p (n t)")
            )
            return codes, scales

        def pick(window, offsets):
            picked = ring.tile([P, offsets.shape[1] * 16], F32, name="picked")
            nc.scalar.activation(picked[:], window.indirect(offsets[:]), ACT.Copy)
            return picked

        def scale_weave_quantise(values, column, name):
            width = values.shape[2]
            woven = keep.tile([P, width, PACK], BF16, name=name + "_woven", align_bytes=64)
            nc.vector.tensor_tensor(
                woven[:].rearrange("p (c i) t -> p c t i", i=RUN),
                values[:].rearrange("p t (c i) -> p c t i", i=RUN),
                cols_sb[:, :, column : column + 1].unsqueeze(1).to_broadcast([P, width // RUN, PACK, RUN]),
                ALU.mult,
            )
            return quantise(woven, name)

        u_mx = []
        for a in range(PASSES):
            gaps = keep.tile([P, PACK, J], F32, name=f"gaps_{a}")
            for g in range(2):
                pair = x_sb[a, g]
                second = pick(pair[:, 0:T], list2)
                nc.vector.tensor_tensor(gaps[:, 2 * g, :], pair[:].indirect(list1[:]), second[:], ALU.subtract)
                second = pick(pair[:, T : 2 * T], list2)
                first = pick(pair[:, T : 2 * T], list1)
                nc.vector.tensor_tensor(gaps[:, 2 * g + 1, :], first[:], second[:], ALU.subtract)
            u_mx.append(scale_weave_quantise(gaps, a, f"u_{a}"))

        bias = keep.tile([P, I // PACK, PACK], F32, name="bias")
        nc.scalar.activation(
            bias[:], bi_bank[:, :, 0 : I // PACK].rearrange("p t n -> p n t"), ACT.Copy, scale=-1.0 / I
        )

        banks = [psum.tile([P, I], F32, name=f"bank_{h}") for h in range(J // P)]

        def multiply(a, v_mx, cols, start, stop):
            u_codes, u_scales = u_mx[a]
            v_codes, v_scales = v_mx
            for h in range(J // P):
                rows = slice(h * P, (h + 1) * P)
                nc.tensor.matmul_mx(
                    out=banks[h][:, cols],
                    lhsT=u_codes[:, rows].bitcast(E5M2X4),
                    lhsT_scale=u_scales[:, rows],
                    rhs=v_codes[:].bitcast(E5M2X4),
                    rhs_scale=v_scales[:],
                    start=start,
                    stop=stop,
                )

        keys = keep.tile([P, PACK, I], F32, name="keys")
        for g in range(2):
            pair = k_first[g]
            nc.vector.tensor_tensor(keys[:, 2 * g, :], pair[:].indirect(list3[:]), own_sb[0][:, 2 * g, :], ALU.add)
            listed = pick(pair[:, V : 2 * V], list3)
            nc.vector.tensor_tensor(keys[:, 2 * g + 1, :], listed[:], own_sb[0][:, 2 * g + 1, :], ALU.add)
        multiply(0, scale_weave_quantise(keys, PASSES, "v_0"), slice(0, I), True, False)

        starts = range(0, I, HALF)
        woven = {c: keep.tile([P, HALF, PACK], BF16, name=f"v_1_woven_{c}", align_bytes=64) for c in starts}
        for t in LAST_ORDER:
            halves = {}
            for c in starts:
                halves[c] = ring.tile([P, HALF], F32, name="half")
                nc.vector.tensor_tensor(
                    halves[c][:],
                    k_last[t][:].indirect(list3[:, c // 16 : (c + HALF) // 16]),
                    own_sb[1][:, t, c : c + HALF],
                    ALU.add,
                )
            factor = cols_sb[:, t, PASSES + 1 : PASSES + 2]
            for c in starts:
                if t >= PACK // 2:
                    nc.vector.tensor_scalar(woven[c][:, :, t], halves[c][:], factor, None, ALU.mult)
                else:
                    nc.scalar.activation(woven[c][:, :, t], halves[c][:], ACT.Copy, scale=factor)
        for c in starts:
            multiply(1, quantise(woven[c], f"v_1_{c}"), slice(c, c + HALF), False, c + HALF == I)

        for h in range(J // P):
            shrunk = keep.tile([P, I], F32, name=f"shrunk_{h}")
            neg_mean = keep.tile([P, 1], F32, name=f"neg_mean_{h}")
            nc.vector.scalar_tensor_tensor(
                shrunk[:], banks[h][:], -1.0 / I, bias[:].rearrange("p n t -> p (n t)"),
                ALU.mult, ALU.add, accum_out=neg_mean[:],
            )
            result = keep.tile([P, I], F32, name=f"result_{h}")
            nc.scalar.activation(result[:], shrunk[:], ACT.Relu, bias=neg_mean[:], scale=-float(I))
            nc.sync.dma_start(out=out[h * P : (h + 1) * P, :], in_=result[:])
